import numpy as np
import ml_dtypes


def mxq(x, axis, fmt="e4m3"):
    dtype, down = {"e4m3": (ml_dtypes.float8_e4m3fn, 7), "e5m2": (ml_dtypes.float8_e5m2, 14)}[fmt]
    v = np.moveaxis(np.asarray(x, np.float32).astype(ml_dtypes.bfloat16).astype(np.float64), axis, -1)
    blocks = v.reshape(v.shape[:-1] + (-1, 32))
    amax = np.abs(blocks).max(-1, keepdims=True)
    byte = np.maximum(np.where(amax > 0, np.frexp(amax)[1] - 1 + 127, 0) - down, 1)
    scale = np.exp2(byte - 127.0)
    codes = (blocks / scale).astype(np.float32).astype(dtype).astype(np.float64)
    return np.moveaxis((codes * scale).reshape(v.shape), -1, axis)


WIDE = False


def mx_kscale(k):
    if not WIDE:
        return np.ones(k)
    levels = np.array([10, -10, 5, -5, 0])
    if k % 512:
        return np.exp2(np.random.permutation(np.resize(levels, k // 32))).repeat(32)
    a = np.empty((k // 512, 16))
    for p in range(k // 512):
        a[p, :8] = np.random.permutation(np.resize(levels, 8))
        for g in range(8):
            far = levels[np.abs(levels - a[p, g]) >= 10]
            a[p, g + 8] = far[np.random.randint(len(far))]
    return np.exp2(a.ravel()).repeat(32)


def f64(x):
    return np.asarray(x).astype(np.float64)


E2M1 = np.array([0.0, 0.5, 1.0, 1.5, 2.0, 3.0, 4.0, 6.0, -0.0, -0.5, -1.0, -1.5, -2.0, -3.0, -4.0, -6.0])


def pack_weight(w, fmt):
    k, n = w.shape
    w = f64(np.asarray(w, np.float32).astype(ml_dtypes.bfloat16)).reshape(k // 32, 32, n)
    amax = np.abs(w).max(1)
    if fmt == "e4m3":
        byte = np.frexp(amax)[1] - 1 + 127 - 7
    else:
        mant, ex = np.frexp(amax / 6.0)
        byte = np.where(mant > 0.5, ex, ex - 1) + 127
    byte = np.clip(np.where(amax > 0, byte, 1), 1, 254)
    scaled = (w * np.exp2(127.0 - byte)[:, None, :]).reshape(k, n).astype(np.float32)
    by_word = np.ascontiguousarray(scaled.reshape(k // 512, 128, 4, n).transpose(0, 1, 3, 2))
    if fmt == "e4m3":
        words = by_word.astype(ml_dtypes.float8_e4m3fn).view(np.uint8)
    else:
        c = by_word.astype(ml_dtypes.float4_e2m1fn).view(np.uint8) & 0xF
        words = (c[..., 0::2] | (c[..., 1::2] << 4)).reshape(k // 512, 128, 2 * n)
    return np.ascontiguousarray(words), np.ascontiguousarray(byte.astype(np.uint8).reshape(k // 512, 16, n))


def unpack_weight(words, scales, fmt):
    g, _, n = scales.shape
    words = np.ascontiguousarray(words).reshape(g, 128, n, -1)
    if fmt == "e4m3":
        vals = words.view(ml_dtypes.float8_e4m3fn).astype(np.float64)
    else:
        nib = np.empty((g, 128, n, 4), np.uint8)
        nib[..., 0::2] = words & 0xF
        nib[..., 1::2] = words >> 4
        vals = E2M1[nib]
    vals = vals * np.repeat(np.exp2(scales.astype(np.float64) - 127.0), 8, axis=1)[..., None]
    return vals.transpose(0, 1, 3, 2).reshape(g * 512, n)


K, L, Q, I = 512, 1024, 512, 1024


def setup_inputs():
    n = np.random.standard_normal
    fk = mx_kscale(K)
    fl = mx_kscale(L)
    qap = pack_weight(n((K, Q)) * np.random.uniform(0.01, 0.1, (1, Q)) * fk[:, None], "e4m3")
    qbp = pack_weight(n((L, Q)) * np.random.uniform(0.005, 0.05, (1, Q)) * fl[:, None], "e2m1")
    kbp = pack_weight(n((L, I)) / fl[:, None], "e4m3")
    return {
        "qa_words": qap[0],
        "qa_scales": qap[1],
        "ka": (n((K, I)) / fk[:, None]).astype(np.float32),
        "qb_words": qbp[0],
        "qb_scales": qbp[1],
        "kb_words": kbp[0],
        "kb_scales": kbp[1],
        "cw1": (np.random.uniform(0.5, 2.0, (1, I))).astype(np.float32),
    }


def reference(qa_words, qa_scales, ka, qb_words, qb_scales, kb_words, kb_scales, cw1):
    qau = unpack_weight(qa_words, qa_scales, "e4m3")
    qbu = unpack_weight(qb_words, qb_scales, "e2m1")
    kbu = unpack_weight(kb_words, kb_scales, "e4m3")
    kaq = mxq(f64(ka), 0, "e4m3")
    a = qau.T @ kaq + qbu.T @ kbu
    e = np.exp(0.7 * a / (np.mean(np.abs(a), axis=1, keepdims=True) + 0.1))
    y = 256.0 * e * f64(cw1) / np.sum(e, axis=1, keepdims=True)
    return y

@@ -1,0 +1,227 @@
+from contextlib import ExitStack
+
+import concourse.mybir as mybir
+from concourse.masks import make_identity
+
+K, L, Q, I = 512, 1024, 512, 1024
+FLOPS = 2 * (K + L) * Q * I
+
+F32 = mybir.dt.float32
+BF16 = mybir.dt.bfloat16
+I32 = mybir.dt.int32
+U32 = mybir.dt.uint32
+U8 = mybir.dt.uint8
+FP8X4 = mybir.dt.float8_e4m3fn_x4
+FP4X4 = mybir.dt.float4_e2m1fn_x4
+ALU = mybir.AluOpType
+ACT = mybir.ActivationFunctionType
+AXIS = mybir.AxisListType
+
+P = 128
+PACK = 4
+TILES = Q // P
+HALF = 512
+QUARTER = 256
+B_PASSES = L // (P * PACK)
+CW_PER_PARTITION = I // P
+SCALAR_COLS = (96, 96, 128, 128)
+
+
+def tile_mix_shares_by_row_scale_kernel(tc, qa_words, qa_scales, ka, qb_words, qb_scales, kb_words, kb_scales, cw1, out):
+    nc = tc.nc
+    with ExitStack() as ctx:
+        sb = ctx.enter_context(tc.tile_pool(name="sb", bufs=1))
+        psum = ctx.enter_context(tc.psum_pool(name="psum", bufs=1))
+        ctx.enter_context(tc.manual_schedule())
+
+        acc = [[psum.tile([P, HALF], F32, name="acc_%d_%d" % (t, h)) for h in range(2)] for t in range(TILES)]
+        qa_w = sb.tile([P, Q], U32, align_bytes=64)
+        qa_s = sb.tile([P, 1, Q], U8, align_bytes=64)
+        qb_w = sb.tile([P, B_PASSES, 2 * Q], U8, align_bytes=64)
+        qb_s = sb.tile([P, B_PASSES, Q], U8, align_bytes=64)
+        kb_s = sb.tile([P, B_PASSES, I], U8, align_bytes=64)
+        kb_first = sb.tile([P, B_PASSES, HALF], U32, align_bytes=64)
+        kb_second = [sb.tile([P, HALF], U32, align_bytes=64, name="kb_second_%d" % z) for z in range(B_PASSES)]
+        ka_raw = [sb.tile([P, PACK, QUARTER], F32, name="ka_raw_%d" % c) for c in range(4)]
+        ka_bf = [sb.tile([P, QUARTER, PACK], BF16, align_bytes=64, name="ka_bf_%d" % c) for c in range(4)]
+        ka_w = sb.tile([P, I], U32, align_bytes=64)
+        ka_s = sb.tile([P, I], U8, align_bytes=64)
+        cw_rows = sb.tile([P, CW_PER_PARTITION], F32)
+        cw_all = sb.tile([P, I], F32)
+        ident = sb.tile([P, P], F32)
+        warm = sb.tile([P, 1], F32)
+        e = [sb.tile([P, I], F32, name="e_%d" % t) for t in range(TILES)]
+        y = [sb.tile([P, I], F32, name="y_%d" % t) for t in range(TILES)]
+        mag = [[sb.tile([P, 1], F32, name="mag_%d_%d" % (t, h)) for h in range(2)] for t in range(TILES)]
+        neg_max = [[sb.tile([P, 1], F32, name="neg_max_%d_%d" % (t, h)) for h in range(2)] for t in range(TILES)]
+        esum = [[sb.tile([P, 1], F32, name="esum_%d_%d" % (t, h)) for h in range(2)] for t in range(TILES)]
+        denom = [sb.tile([P, 1], F32, name="denom_%d" % t) for t in range(TILES)]
+        sharp = [sb.tile([P, 1], F32, name="sharp_%d" % t) for t in range(TILES)]
+        shift = [sb.tile([P, 1], F32, name="shift_%d" % t) for t in range(TILES)]
+        total = [sb.tile([P, 1], F32, name="total_%d" % t) for t in range(TILES)]
+        inv = [sb.tile([P, 1], F32, name="inv_%d" % t) for t in range(TILES)]
+
+        def cols(n, width):
+            return slice(n * width, (n + 1) * width)
+
+        def load_scales(plane, scales, row_range):
+            rows = scales.rearrange("z (q r) n -> r q z n", r=4)
+            for r in row_range:
+                nc.sync.dma_start(out=plane[r:P:32, :, :].bitcast(I32), in_=rows[r].bitcast(I32))
+
+        def load_ka(c):
+            nc.sync.dma_start(out=ka_raw[c][:], in_=ka[:, cols(c, QUARTER)].rearrange("(p j) w -> p j w", j=PACK))
+
+        kb_by_partition = kb_words.rearrange("z p n t -> p z (n t)").bitcast(I32)
+
+        def interleave(copy, c, lo, hi):
+            copy(
+                out=ka_bf[c][:, lo:hi, :].rearrange("p (g w) j -> p g j w", w=4),
+                in_=ka_raw[c][:, :, lo:hi].rearrange("p j (g w) -> p g j w", w=4),
+            )
+
+        def cast_scalar(c):
+            interleave(nc.scalar.copy, c, 0, SCALAR_COLS[c])
+
+        def cast_vector(c):
+            interleave(nc.vector.tensor_copy, c, SCALAR_COLS[c], QUARTER)
+
+        def quantize(c):
+            nc.vector.quantize_mx(
+                out=ka_w[:, cols(c, QUARTER)].bitcast(FP8X4),
+                scales=ka_s[:, cols(c, QUARTER)],
+                in_=ka_bf[c][:].rearrange("p w j -> p (w j)"),
+            )
+
+        def pass_a(t, c, start, stop):
+            nc.tensor.matmul_mx(
+                out=acc[t][c // 2][:, cols(c % 2, QUARTER)],
+                lhsT=qa_w[:, cols(t, P)].bitcast(FP8X4),
+                lhsT_scale=qa_s[:, 0, cols(t, P)],
+                rhs=ka_w[:, cols(c, QUARTER)].bitcast(FP8X4),
+                rhs_scale=ka_s[:, cols(c, QUARTER)],
+                start=start,
+                stop=stop,
+            )
+
+        def pass_b(t, h, z, start, stop):
+            words = kb_first[:, z, :] if h == 0 else kb_second[z][:]
+            nc.tensor.matmul_mx(
+                out=acc[t][h][:],
+                lhsT=qb_w[:, z, cols(t, 2 * P)].bitcast(FP4X4),
+                lhsT_scale=qb_s[:, z, cols(t, P)],
+                rhs=words.bitcast(FP8X4),
+                rhs_scale=kb_s[:, z, cols(h, HALF)],
+                start=start,
+                stop=stop,
+            )
+
+        def magnitude(t, h):
+            nc.scalar.activation(
+                out=e[t][:, cols(h, HALF)], in_=acc[t][h][:], func=ACT.Abs, scale=1.0 / (0.7 * I), accum_out=mag[t][h][:]
+            )
+
+        def row_max(t, h):
+            nc.vector.tensor_reduce(out=neg_max[t][h][:], in_=acc[t][h][:], axis=AXIS.X, op=ALU.max, negate=True)
+
+        def sharpness(t):
+            nc.vector.tensor_scalar(
+                out=denom[t][:], in0=mag[t][1][:], scalar1=mag[t][0][:], scalar2=0.1 / 0.7, op0=ALU.add, op1=ALU.add
+            )
+            row_max(t, 1)
+            nc.vector.reciprocal(out=sharp[t][:], in_=denom[t][:])
+            nc.vector.tensor_scalar(
+                out=shift[t][:], in0=neg_max[t][1][:], scalar1=neg_max[t][0][:], scalar2=sharp[t][:], op0=ALU.min, op1=ALU.mult
+            )
+
+        def exponentials(t):
+            for h in range(2):
+                nc.scalar.activation(
+                    out=e[t][:, cols(h, HALF)], in_=acc[t][h][:], func=ACT.Exp, scale=sharp[t][:], bias=shift[t][:], accum_out=esum[t][h][:]
+                )
+
+        def shares(t, pieces):
+            nc.vector.tensor_tensor(out=total[t][:], in0=esum[t][0][:], in1=esum[t][1][:], op=ALU.add)
+            nc.vector.reciprocal(out=inv[t][:], in_=total[t][:])
+            width = I // pieces
+            for n in range(pieces):
+                nc.vector.scalar_tensor_tensor(
+                    out=y[t][:, cols(n, width)], in0=e[t][:, cols(n, width)], scalar=inv[t][:], in1=cw_all[:, cols(n, width)], op0=ALU.mult, op1=ALU.mult
+                )
+                nc.sync.dma_start(out=out[cols(t, P), cols(n, width)], in_=y[t][:, cols(n, width)])
+
+        for plane in (qb_s, kb_s, qa_s):
+            nc.vector.memset(plane[:].bitcast(I32), 0)
+        nc.vector.memset(warm[:], 0.0)
+        nc.scalar.activation(out=warm[:], in_=warm[:], func=ACT.Exp)
+        nc.gpsimd.dma_start(out=cw_rows[:], in_=cw1.rearrange("o (p m) -> p (o m)", p=P))
+        make_identity(nc, ident[:])
+
+        nc.sync.dma_start(out=qb_w[:].bitcast(I32), in_=qb_words.rearrange("z p b -> p z b").bitcast(I32))
+        nc.sync.dma_start(out=kb_first[:].bitcast(I32), in_=kb_by_partition[:, :, cols(0, HALF)])
+        load_scales(qb_s, qb_scales, range(4))
+        load_scales(kb_s, kb_scales, range(2))
+        load_ka(0)
+        load_scales(kb_s, kb_scales, range(2, 4))
+        load_ka(1)
+        load_scales(qa_s, qa_scales, range(4))
+        nc.sync.dma_start(out=qa_w[:].bitcast(I32), in_=qa_words.rearrange("z p n t -> p (z n t)").bitcast(I32))
+        load_ka(2)
+        load_ka(3)
+        for z in range(B_PASSES):
+            nc.sync.dma_start(out=kb_second[z][:].bitcast(I32), in_=kb_by_partition[:, z, cols(1, HALF)])
+
+        cw_view = cw_all[:].rearrange("p (n m) -> p n m", m=CW_PER_PARTITION)
+        for b in range(2):
+            bank = acc[TILES - 1 - b][1]
+            for j in range(4):
+                m = 4 * b + j
+                nc.tensor.transpose(bank[:, cols(j, P)], cw_rows[:, m : m + 1].to_broadcast([P, P]), ident[:])
+            nc.scalar.activation(
+                out=cw_view[:, :, cols(b, 4)], in_=bank[:].rearrange("p (j n) -> p n j", j=4), func=ACT.Copy, scale=256.0
+            )
+
+        for c in range(2):
+            cast_scalar(c)
+            cast_vector(c)
+            quantize(c)
+        for t in range(2):
+            for z in range(B_PASSES):
+                pass_b(t, 0, z, z == 0, False)
+        for t in range(TILES):
+            if t >= 2:
+                for z in range(B_PASSES):
+                    pass_b(t, 0, z, z == 0, False)
+            for c in range(2):
+                pass_a(t, c, False, c == 1)
+        magnitude(0, 0)
+        row_max(0, 0)
+        magnitude(1, 0)
+        cast_scalar(2)
+        cast_vector(2)
+        row_max(1, 0)
+        quantize(2)
+        magnitude(2, 0)
+        cast_scalar(3)
+        cast_vector(3)
+        row_max(2, 0)
+        quantize(3)
+        magnitude(3, 0)
+        row_max(3, 0)
+
+        for c in (2, 3):
+            for t in range(TILES):
+                pass_a(t, c, c == 2, False)
+        for t in range(TILES):
+            for z in range(B_PASSES):
+                pass_b(t, 1, z, False, z == B_PASSES - 1)
+        for t in range(3):
+            magnitude(t, 1)
+            sharpness(t)
+        exponentials(0)
+        magnitude(3, 1)
+        sharpness(3)
+        shares(0, 2)
+        for t in range(1, TILES):
+            exponentials(t)
+            shares(t, 2 if t < TILES - 1 else 4)

@@ -22,9 +22,9 @@ PACK = 4
 TILES = Q // P
 HALF = 512
 QUARTER = 256
+STEPS = I // QUARTER
 B_PASSES = L // (P * PACK)
-CW_PER_PARTITION = I // P
-SCALAR_COLS = (96, 96, 128, 128)
+SCALAR_COLS = (80, 96, 96, 96)
 
 
 def tile_mix_shares_by_row_scale_kernel(tc, qa_words, qa_scales, ka, qb_words, qb_scales, kb_words, kb_scales, cw1, out):
@@ -40,188 +40,259 @@ def tile_mix_shares_by_row_scale_kernel(tc, qa_words, qa_scales, ka, qb_words, q
         qb_w = sb.tile([P, B_PASSES, 2 * Q], U8, align_bytes=64)
         qb_s = sb.tile([P, B_PASSES, Q], U8, align_bytes=64)
         kb_s = sb.tile([P, B_PASSES, I], U8, align_bytes=64)
-        kb_first = sb.tile([P, B_PASSES, HALF], U32, align_bytes=64)
-        kb_second = [sb.tile([P, HALF], U32, align_bytes=64, name="kb_second_%d" % z) for z in range(B_PASSES)]
-        ka_raw = [sb.tile([P, PACK, QUARTER], F32, name="ka_raw_%d" % c) for c in range(4)]
-        ka_bf = [sb.tile([P, QUARTER, PACK], BF16, align_bytes=64, name="ka_bf_%d" % c) for c in range(4)]
-        ka_w = sb.tile([P, I], U32, align_bytes=64)
-        ka_s = sb.tile([P, I], U8, align_bytes=64)
-        cw_rows = sb.tile([P, CW_PER_PARTITION], F32)
-        cw_all = sb.tile([P, I], F32)
+        kb_w = [sb.tile([P, B_PASSES, QUARTER], U32, align_bytes=64, name="kb_w_%d" % s) for s in range(STEPS)]
+        ka_raw = [sb.tile([P, PACK, QUARTER], F32, name="ka_raw_%d" % s) for s in range(STEPS)]
+        ka_bf = [sb.tile([P, QUARTER, PACK], BF16, align_bytes=64, name="ka_bf_%d" % s) for s in range(STEPS)]
+        ka_w = [sb.tile([P, QUARTER], U32, align_bytes=64, name="ka_w_%d" % s) for s in range(STEPS)]
+        ka_s = [sb.tile([P, QUARTER], U8, align_bytes=64, name="ka_s_%d" % s) for s in range(STEPS)]
+        cw_rows = sb.tile([P, P], F32)
+        cw_cols = sb.tile([P, I // P], F32)
+        cw_first = sb.tile([P, QUARTER], F32)
         ident = sb.tile([P, P], F32)
+        ones = sb.tile([P, TILES, 1], F32)
         warm = sb.tile([P, 1], F32)
-        e = [sb.tile([P, I], F32, name="e_%d" % t) for t in range(TILES)]
-        y = [sb.tile([P, I], F32, name="y_%d" % t) for t in range(TILES)]
-        mag = [[sb.tile([P, 1], F32, name="mag_%d_%d" % (t, h)) for h in range(2)] for t in range(TILES)]
-        neg_max = [[sb.tile([P, 1], F32, name="neg_max_%d_%d" % (t, h)) for h in range(2)] for t in range(TILES)]
+        e = [[sb.tile([P, HALF], F32, name="e_%d_%d" % (t, h)) for h in range(2)] for t in range(TILES)]
+        y = [[sb.tile([P, HALF], F32, name="y_%d_%d" % (t, h)) for h in range(2)] for t in range(TILES)]
+        weighted = [sb.tile([P, QUARTER], F32, name="weighted_%d" % t) for t in range(TILES)]
+        mag = sb.tile([P, TILES, STEPS + 1], F32)
+        neg_max = sb.tile([P, TILES, STEPS], F32)
+        neg_max_row = sb.tile([P, TILES], F32)
+        denom = sb.tile([P, TILES], F32)
+        sharp = sb.tile([P, TILES], F32)
+        shift = sb.tile([P, TILES], F32)
         esum = [[sb.tile([P, 1], F32, name="esum_%d_%d" % (t, h)) for h in range(2)] for t in range(TILES)]
-        denom = [sb.tile([P, 1], F32, name="denom_%d" % t) for t in range(TILES)]
-        sharp = [sb.tile([P, 1], F32, name="sharp_%d" % t) for t in range(TILES)]
-        shift = [sb.tile([P, 1], F32, name="shift_%d" % t) for t in range(TILES)]
         total = [sb.tile([P, 1], F32, name="total_%d" % t) for t in range(TILES)]
         inv = [sb.tile([P, 1], F32, name="inv_%d" % t) for t in range(TILES)]
 
         def cols(n, width):
             return slice(n * width, (n + 1) * width)
 
-        def load_scales(plane, scales, row_range):
-            rows = scales.rearrange("z (q r) n -> r q z n", r=4)
-            for r in row_range:
-                nc.sync.dma_start(out=plane[r:P:32, :, :].bitcast(I32), in_=rows[r].bitcast(I32))
+        def quarter(s):
+            return 2 * (s % 2) + s // 2
 
-        def load_ka(c):
-            nc.sync.dma_start(out=ka_raw[c][:], in_=ka[:, cols(c, QUARTER)].rearrange("(p j) w -> p j w", j=PACK))
+        def scores(t, s):
+            return acc[t][s % 2][:, cols(s // 2, QUARTER)]
+
+        def load_scales(queue, plane, scales):
+            rows = scales.rearrange("z (q r) n -> r q z n", r=4)
+            for r in range(4):
+                queue.dma_start(out=plane[r:P:32, :, :].bitcast(I32), in_=rows[r].bitcast(I32))
+
+        def load_ka(s):
+            nc.sync.dma_start(out=ka_raw[s][:], in_=ka[:, cols(quarter(s), QUARTER)].rearrange("(p j) w -> p j w", j=PACK))
 
         kb_by_partition = kb_words.rearrange("z p n t -> p z (n t)").bitcast(I32)
 
-        def interleave(copy, c, lo, hi):
+        def load_kb(s):
+            nc.sync.dma_start(out=kb_w[s][:].bitcast(I32), in_=kb_by_partition[:, :, cols(quarter(s), QUARTER)])
+
+        def interleave(copy, s, lo, hi):
             copy(
-                out=ka_bf[c][:, lo:hi, :].rearrange("p (g w) j -> p g j w", w=4),
-                in_=ka_raw[c][:, :, lo:hi].rearrange("p j (g w) -> p g j w", w=4),
+                out=ka_bf[s][:, lo:hi, :].rearrange("p (g w) j -> p g j w", w=4),
+                in_=ka_raw[s][:, :, lo:hi].rearrange("p j (g w) -> p g j w", w=4),
             )
 
-        def cast_scalar(c):
-            interleave(nc.scalar.copy, c, 0, SCALAR_COLS[c])
+        def cast_scalar(s):
+            interleave(nc.scalar.copy, s, 0, SCALAR_COLS[s])
 
-        def cast_vector(c):
-            interleave(nc.vector.tensor_copy, c, SCALAR_COLS[c], QUARTER)
+        def cast_vector(s):
+            interleave(nc.vector.tensor_copy, s, SCALAR_COLS[s], QUARTER)
 
-        def quantize(c):
-            nc.vector.quantize_mx(
-                out=ka_w[:, cols(c, QUARTER)].bitcast(FP8X4),
-                scales=ka_s[:, cols(c, QUARTER)],
-                in_=ka_bf[c][:].rearrange("p w j -> p (w j)"),
-            )
+        def quantize(s):
+            nc.vector.quantize_mx(out=ka_w[s][:].bitcast(FP8X4), scales=ka_s[s][:], in_=ka_bf[s][:].rearrange("p w j -> p (w j)"))
 
-        def pass_a(t, c, start, stop):
+        def pass_a(t, s, start, stop):
             nc.tensor.matmul_mx(
-                out=acc[t][c // 2][:, cols(c % 2, QUARTER)],
+                out=scores(t, s),
                 lhsT=qa_w[:, cols(t, P)].bitcast(FP8X4),
                 lhsT_scale=qa_s[:, 0, cols(t, P)],
-                rhs=ka_w[:, cols(c, QUARTER)].bitcast(FP8X4),
-                rhs_scale=ka_s[:, cols(c, QUARTER)],
+                rhs=ka_w[s][:].bitcast(FP8X4),
+                rhs_scale=ka_s[s][:],
                 start=start,
                 stop=stop,
             )
 
-        def pass_b(t, h, z, start, stop):
-            words = kb_first[:, z, :] if h == 0 else kb_second[z][:]
-            nc.tensor.matmul_mx(
-                out=acc[t][h][:],
-                lhsT=qb_w[:, z, cols(t, 2 * P)].bitcast(FP4X4),
-                lhsT_scale=qb_s[:, z, cols(t, P)],
-                rhs=words.bitcast(FP8X4),
-                rhs_scale=kb_s[:, z, cols(h, HALF)],
-                start=start,
-                stop=stop,
-            )
+        def passes_b(t, s, start, stop):
+            for z in range(B_PASSES):
+                for u in range(2):
+                    nc.tensor.matmul_mx(
+                        out=scores(t, s)[:, cols(u, P)],
+                        lhsT=qb_w[:, z, cols(t, 2 * P)].bitcast(FP4X4),
+                        lhsT_scale=qb_s[:, z, cols(t, P)],
+                        rhs=kb_w[s][:, z, cols(u, P)].bitcast(FP8X4),
+                        rhs_scale=kb_s[:, z, cols(2 * quarter(s) + u, P)],
+                        start=start and z == 0 and u == 0,
+                        stop=stop and z == B_PASSES - 1 and u == 1,
+                    )
 
-        def magnitude(t, h):
+        def magnitude(t, s):
             nc.scalar.activation(
-                out=e[t][:, cols(h, HALF)], in_=acc[t][h][:], func=ACT.Abs, scale=1.0 / (0.7 * I), accum_out=mag[t][h][:]
+                out=e[t][s % 2][:, cols(s // 2, QUARTER)], in_=scores(t, s), func=ACT.Abs, scale=1.0 / (0.7 * I), accum_out=mag[:, t, s : s + 1]
             )
 
-        def row_max(t, h):
-            nc.vector.tensor_reduce(out=neg_max[t][h][:], in_=acc[t][h][:], axis=AXIS.X, op=ALU.max, negate=True)
+        def row_max(t, s):
+            nc.vector.tensor_reduce(out=neg_max[:, t, s : s + 1], in_=scores(t, s), axis=AXIS.X, op=ALU.max, negate=True)
 
-        def sharpness(t):
+        def denominator(lo, hi):
+            nc.vector.tensor_reduce(out=denom[:, lo:hi], in_=mag[:, lo:hi, :], axis=AXIS.X, op=ALU.add)
+
+        def join_maxima(lo, hi):
+            nc.vector.tensor_reduce(out=neg_max_row[:, lo:hi], in_=neg_max[:, lo:hi, :], axis=AXIS.X, op=ALU.min)
+
+        def join_early_maxima(t):
+            nc.vector.tensor_reduce(out=neg_max_row[:, t : t + 1], in_=neg_max[:, t, : STEPS - 1], axis=AXIS.X, op=ALU.min)
+
+        def first_shift(t):
             nc.vector.tensor_scalar(
-                out=denom[t][:], in0=mag[t][1][:], scalar1=mag[t][0][:], scalar2=0.1 / 0.7, op0=ALU.add, op1=ALU.add
+                out=shift[:, t : t + 1], in0=neg_max[:, t, STEPS - 1 :], scalar1=neg_max_row[:, t : t + 1], scalar2=sharp[:, t : t + 1], op0=ALU.min, op1=ALU.mult
             )
-            row_max(t, 1)
-            nc.vector.reciprocal(out=sharp[t][:], in_=denom[t][:])
+
+        def shifts(lo, hi):
+            nc.vector.tensor_tensor(out=shift[:, lo:hi], in0=neg_max_row[:, lo:hi], in1=sharp[:, lo:hi], op=ALU.mult)
+
+        def sharpness(lo, hi):
+            nc.vector.reciprocal(out=sharp[:, lo:hi], in_=denom[:, lo:hi])
+
+        def exponential(t, h):
+            nc.scalar.activation(
+                out=e[t][h][:], in_=acc[t][h][:], func=ACT.Exp, scale=sharp[:, t : t + 1], bias=shift[:, t : t + 1], accum_out=esum[t][h][:]
+            )
+
+        def add_halves(t):
             nc.vector.tensor_scalar(
-                out=shift[t][:], in0=neg_max[t][1][:], scalar1=neg_max[t][0][:], scalar2=sharp[t][:], op0=ALU.min, op1=ALU.mult
+                out=total[t][:], in0=esum[t][1][:], scalar1=esum[t][0][:], scalar2=1.0 / 256.0, op0=ALU.add, op1=ALU.mult
             )
 
-        def exponentials(t):
-            for h in range(2):
-                nc.scalar.activation(
-                    out=e[t][:, cols(h, HALF)], in_=acc[t][h][:], func=ACT.Exp, scale=sharp[t][:], bias=shift[t][:], accum_out=esum[t][h][:]
-                )
-
-        def shares(t, pieces):
-            nc.vector.tensor_tensor(out=total[t][:], in0=esum[t][0][:], in1=esum[t][1][:], op=ALU.add)
+        def invert(t):
             nc.vector.reciprocal(out=inv[t][:], in_=total[t][:])
-            width = I // pieces
-            for n in range(pieces):
-                nc.vector.scalar_tensor_tensor(
-                    out=y[t][:, cols(n, width)], in0=e[t][:, cols(n, width)], scalar=inv[t][:], in1=cw_all[:, cols(n, width)], op0=ALU.mult, op1=ALU.mult
-                )
-                nc.sync.dma_start(out=out[cols(t, P), cols(n, width)], in_=y[t][:, cols(n, width)])
 
-        for plane in (qb_s, kb_s, qa_s):
-            nc.vector.memset(plane[:].bitcast(I32), 0)
-        nc.vector.memset(warm[:], 0.0)
-        nc.scalar.activation(out=warm[:], in_=warm[:], func=ACT.Exp)
-        nc.gpsimd.dma_start(out=cw_rows[:], in_=cw1.rearrange("o (p m) -> p (o m)", p=P))
-        make_identity(nc, ident[:])
+        def spread_cw(bank, first_block, blocks):
+            for j in range(blocks):
+                m = first_block + j
+                nc.tensor.transpose(bank[:, cols(j, P)], cw_cols[:, m : m + 1].to_broadcast([P, P]), ident[:])
 
-        nc.sync.dma_start(out=qb_w[:].bitcast(I32), in_=qb_words.rearrange("z p b -> p z b").bitcast(I32))
-        nc.sync.dma_start(out=kb_first[:].bitcast(I32), in_=kb_by_partition[:, :, cols(0, HALF)])
-        load_scales(qb_s, qb_scales, range(4))
-        load_scales(kb_s, kb_scales, range(2))
-        load_ka(0)
-        load_scales(kb_s, kb_scales, range(2, 4))
-        load_ka(1)
-        load_scales(qa_s, qa_scales, range(4))
-        nc.sync.dma_start(out=qa_w[:].bitcast(I32), in_=qa_words.rearrange("z p n t -> p (z n t)").bitcast(I32))
-        load_ka(2)
-        load_ka(3)
-        for z in range(B_PASSES):
-            nc.sync.dma_start(out=kb_second[z][:].bitcast(I32), in_=kb_by_partition[:, z, cols(1, HALF)])
-
-        cw_view = cw_all[:].rearrange("p (n m) -> p n m", m=CW_PER_PARTITION)
-        for b in range(2):
-            bank = acc[TILES - 1 - b][1]
-            for j in range(4):
-                m = 4 * b + j
-                nc.tensor.transpose(bank[:, cols(j, P)], cw_rows[:, m : m + 1].to_broadcast([P, P]), ident[:])
-            nc.scalar.activation(
-                out=cw_view[:, :, cols(b, 4)], in_=bank[:].rearrange("p (j n) -> p n j", j=4), func=ACT.Copy, scale=256.0
+        def shares(t, h, lo, hi, cw_ap):
+            nc.vector.scalar_tensor_tensor(
+                out=y[t][h][:, lo:hi], in0=e[t][h][:, lo:hi], scalar=inv[t][:], in1=cw_ap, op0=ALU.mult, op1=ALU.mult
             )
 
-        for c in range(2):
-            cast_scalar(c)
-            cast_vector(c)
-            quantize(c)
-        for t in range(2):
-            for z in range(B_PASSES):
-                pass_b(t, 0, z, z == 0, False)
-        for t in range(TILES):
-            if t >= 2:
-                for z in range(B_PASSES):
-                    pass_b(t, 0, z, z == 0, False)
-            for c in range(2):
-                pass_a(t, c, False, c == 1)
-        magnitude(0, 0)
-        row_max(0, 0)
-        magnitude(1, 0)
-        cast_scalar(2)
-        cast_vector(2)
-        row_max(1, 0)
-        quantize(2)
-        magnitude(2, 0)
-        cast_scalar(3)
-        cast_vector(3)
-        row_max(2, 0)
-        quantize(3)
-        magnitude(3, 0)
-        row_max(3, 0)
+        def weigh_first(t):
+            nc.gpsimd.tensor_tensor(out=weighted[t][:], in0=e[t][0][:, :QUARTER], in1=cw_first[:], op=ALU.mult)
 
-        for c in (2, 3):
-            for t in range(TILES):
-                pass_a(t, c, c == 2, False)
+        def shares_first(t):
+            nc.gpsimd.tensor_scalar(
+                out=y[t][0][:, :QUARTER], in0=weighted[t][:], scalar1=inv[t][:], scalar2=0.0, op0=ALU.mult, op1=ALU.add
+            )
+
+        def store(t, h, lo, hi):
+            nc.sync.dma_start(out=out[cols(t, P), h * HALF + lo : h * HALF + hi], in_=y[t][h][:, lo:hi])
+
+        nc.vector.memset(qa_s[:].bitcast(I32), 0)
+        nc.vector.memset(cw_rows[:], 0.0)
+        nc.vector.memset(kb_s[:].bitcast(I32), 0)
+        nc.vector.memset(qb_s[:].bitcast(I32), 0)
+        nc.vector.memset(ones[:], 1.0)
+        nc.scalar.activation(out=warm[:], in_=ones[:, 0, :], func=ACT.Exp)
+        make_identity(nc, ident[:])
+        nc.gpsimd.dma_start(out=cw_rows[: I // P, :], in_=cw1.rearrange("o (m p) -> (o m) p", p=P))
+        load_scales(nc.gpsimd, kb_s, kb_scales)
+
+        load_ka(0)
+        load_scales(nc.sync, qa_s, qa_scales)
+        nc.sync.dma_start(out=qa_w[:].bitcast(I32), in_=qa_words.rearrange("z p n t -> p (z n t)").bitcast(I32))
+        nc.sync.dma_start(out=qb_w[:].bitcast(I32), in_=qb_words.rearrange("z p b -> p z b").bitcast(I32))
+        load_kb(0)
+        load_scales(nc.sync, qb_s, qb_scales)
+        for s in range(1, STEPS):
+            load_ka(s)
+            load_kb(s)
+
+        nc.scalar.activation(out=mag[:, :, STEPS:], in_=ones[:], func=ACT.Copy, scale=0.1 / 0.7)
+        cast_scalar(0)
+        cast_vector(0)
+        quantize(0)
+        nc.tensor.transpose(acc[2][1][:, :P], cw_rows[:], ident[:])
+        nc.scalar.copy(out=cw_cols[:], in_=acc[2][1][:, : I // P])
+        spread_cw(acc[3][1], 0, 2)
+        nc.scalar.copy(out=cw_first[:], in_=acc[3][1][:, :QUARTER])
         for t in range(TILES):
-            for z in range(B_PASSES):
-                pass_b(t, 1, z, False, z == B_PASSES - 1)
+            pass_a(t, 0, True, False)
+        for t in range(TILES):
+            passes_b(t, 0, False, True)
+        last = STEPS - 1
+        for s in range(1, STEPS):
+            cast_scalar(s)
+            cast_vector(s)
+            if s > 1:
+                row_max(3, s - 2)
+            quantize(s)
+            for t in range(TILES):
+                passes_b(t, s, True, False)
+                pass_a(t, s, False, True)
+            if s < last:
+                for t in range(TILES):
+                    magnitude(t, s - 1)
+                    if t < 3:
+                        row_max(t, s - 1)
         for t in range(3):
-            magnitude(t, 1)
-            sharpness(t)
-        exponentials(0)
-        magnitude(3, 1)
-        sharpness(3)
-        shares(0, 2)
-        for t in range(1, TILES):
-            exponentials(t)
-            shares(t, 2 if t < TILES - 1 else 4)
+            magnitude(t, last - 1)
+            row_max(t, last - 1)
+        join_early_maxima(0)
+        magnitude(0, last)
+        denominator(0, 1)
+        row_max(0, last)
+        sharpness(0, 1)
+        magnitude(3, last - 1)
+        magnitude(1, last)
+        first_shift(0)
+        magnitude(2, last)
+        row_max(1, last)
+        row_max(2, last)
+        exponential(0, 0)
+        exponential(0, 1)
+        spread_cw(acc[0][0], 4, 4)
+        spread_cw(acc[0][1], 2, 2)
+        denominator(1, 3)
+        row_max(3, last)
+        magnitude(3, last)
+        sharpness(1, 3)
+        join_maxima(1, 3)
+        row_max(3, last - 1)
+        shifts(1, 3)
+        for t in (1, 2):
+            exponential(t, 0)
+            exponential(t, 1)
+        add_halves(0)
+        join_maxima(3, 4)
+        invert(0)
+        denominator(3, 4)
+        weigh_first(0)
+        shares_first(0)
+        shares(0, 1, 0, HALF, acc[0][0][:])
+        store(0, 1, 0, HALF)
+        sharpness(3, 4)
+        shares(0, 0, QUARTER, HALF, acc[0][1][:, :QUARTER])
+        store(0, 0, 0, HALF)
+        add_halves(1)
+        shifts(3, 4)
+        invert(1)
+        exponential(3, 0)
+        exponential(3, 1)
+        for t in (1, 2):
+            weigh_first(t)
+            shares_first(t)
+            shares(t, 1, 0, HALF, acc[0][0][:])
+            store(t, 1, 0, HALF)
+            add_halves(t + 1)
+            shares(t, 0, QUARTER, HALF, acc[0][1][:, :QUARTER])
+            store(t, 0, 0, HALF)
+            invert(t + 1)
+        t = TILES - 1
+        weigh_first(t)
+        shares_first(t)
+        for g in range(2):
+            shares(t, 1, g * QUARTER, (g + 1) * QUARTER, acc[0][0][:, cols(g, QUARTER)])
+            store(t, 1, g * QUARTER, (g + 1) * QUARTER)
+        store(t, 0, 0, QUARTER)
+        shares(t, 0, QUARTER, HALF, acc[0][1][:, :QUARTER])
+        store(t, 0, QUARTER, HALF)

@@ -45,8 +45,7 @@ def tile_mix_shares_by_row_scale_kernel(tc, qa_words, qa_scales, ka, qb_words, q
         ka_bf = [sb.tile([P, QUARTER, PACK], BF16, align_bytes=64, name="ka_bf_%d" % s) for s in range(STEPS)]
         ka_w = [sb.tile([P, QUARTER], U32, align_bytes=64, name="ka_w_%d" % s) for s in range(STEPS)]
         ka_s = [sb.tile([P, QUARTER], U8, align_bytes=64, name="ka_s_%d" % s) for s in range(STEPS)]
-        cw_rows = sb.tile([P, P], F32)
-        cw_cols = sb.tile([P, I // P], F32)
+        cw_cols = sb.tile([P, 2, 4], F32)
         cw_first = sb.tile([P, QUARTER], F32)
         ident = sb.tile([P, P], F32)
         ones = sb.tile([P, TILES, 1], F32)
@@ -73,9 +72,9 @@ def tile_mix_shares_by_row_scale_kernel(tc, qa_words, qa_scales, ka, qb_words, q
         def scores(t, s):
             return acc[t][s % 2][:, cols(s // 2, QUARTER)]
 
-        def load_scales(queue, plane, scales):
+        def load_scales(queue, plane, scales, first, last):
             rows = scales.rearrange("z (q r) n -> r q z n", r=4)
-            for r in range(4):
+            for r in range(first, last):
                 queue.dma_start(out=plane[r:P:32, :, :].bitcast(I32), in_=rows[r].bitcast(I32))
 
         def load_ka(s):
@@ -148,7 +147,10 @@ def tile_mix_shares_by_row_scale_kernel(tc, qa_words, qa_scales, ka, qb_words, q
             )
 
         def shifts(lo, hi):
-            nc.vector.tensor_tensor(out=shift[:, lo:hi], in0=neg_max_row[:, lo:hi], in1=sharp[:, lo:hi], op=ALU.mult)
+            for t in range(lo, hi):
+                nc.vector.tensor_scalar(
+                    out=shift[:, t : t + 1], in0=neg_max_row[:, t : t + 1], scalar1=sharp[:, t : t + 1], scalar2=None, op0=ALU.mult
+                )
 
         def sharpness(lo, hi):
             nc.vector.reciprocal(out=sharp[:, lo:hi], in_=denom[:, lo:hi])
@@ -166,14 +168,19 @@ def tile_mix_shares_by_row_scale_kernel(tc, qa_words, qa_scales, ka, qb_words, q
         def invert(t):
             nc.vector.reciprocal(out=inv[t][:], in_=total[t][:])
 
-        def spread_cw(bank, first_block, blocks):
-            for j in range(blocks):
-                m = first_block + j
-                nc.tensor.transpose(bank[:, cols(j, P)], cw_cols[:, m : m + 1].to_broadcast([P, P]), ident[:])
+        def spread_cw(bank, h):
+            for j in range(4):
+                nc.tensor.transpose(bank[:, cols(j, P)], cw_cols[:, h, j : j + 1].to_broadcast([P, P]), ident[:])
 
-        def shares(t, h, lo, hi, cw_ap):
+        def shares(t, h, lo, hi):
+            cw_bank = acc[0][1 - h][:].rearrange("p (j n) -> p n j", j=4)
             nc.vector.scalar_tensor_tensor(
-                out=y[t][h][:, lo:hi], in0=e[t][h][:, lo:hi], scalar=inv[t][:], in1=cw_ap, op0=ALU.mult, op1=ALU.mult
+                out=y[t][h][:, lo:hi].rearrange("p (n j) -> p n j", j=4),
+                in0=e[t][h][:, lo:hi].rearrange("p (n j) -> p n j", j=4),
+                scalar=inv[t][:],
+                in1=cw_bank[:, lo // 4 : hi // 4, :],
+                op0=ALU.mult,
+                op1=ALU.mult,
             )
 
         def weigh_first(t):
@@ -187,34 +194,33 @@ def tile_mix_shares_by_row_scale_kernel(tc, qa_words, qa_scales, ka, qb_words, q
         def store(t, h, lo, hi):
             nc.sync.dma_start(out=out[cols(t, P), h * HALF + lo : h * HALF + hi], in_=y[t][h][:, lo:hi])
 
-        nc.vector.memset(qa_s[:].bitcast(I32), 0)
-        nc.vector.memset(cw_rows[:], 0.0)
-        nc.vector.memset(kb_s[:].bitcast(I32), 0)
-        nc.vector.memset(qb_s[:].bitcast(I32), 0)
+        nc.gpsimd.memset(qb_s[:].bitcast(I32), 0)
+        for plane in (qa_s, kb_s):
+            nc.vector.memset(plane[:].bitcast(I32), 0)
+        load_scales(nc.gpsimd, qb_s, qb_scales, 3, 4)
+        make_identity(nc, ident[:])
         nc.vector.memset(ones[:], 1.0)
         nc.scalar.activation(out=warm[:], in_=ones[:, 0, :], func=ACT.Exp)
-        make_identity(nc, ident[:])
-        nc.gpsimd.dma_start(out=cw_rows[: I // P, :], in_=cw1.rearrange("o (m p) -> (o m) p", p=P))
-        load_scales(nc.gpsimd, kb_s, kb_scales)
 
-        load_ka(0)
-        load_scales(nc.sync, qa_s, qa_scales)
         nc.sync.dma_start(out=qa_w[:].bitcast(I32), in_=qa_words.rearrange("z p n t -> p (z n t)").bitcast(I32))
-        nc.sync.dma_start(out=qb_w[:].bitcast(I32), in_=qb_words.rearrange("z p b -> p z b").bitcast(I32))
+        load_scales(nc.sync, qa_s, qa_scales, 0, 4)
+        load_scales(nc.sync, kb_s, kb_scales, 0, 2)
+        load_ka(0)
         load_kb(0)
-        load_scales(nc.sync, qb_s, qb_scales)
+        nc.sync.dma_start(out=qb_w[:].bitcast(I32), in_=qb_words.rearrange("z p b -> p z b").bitcast(I32))
+        load_scales(nc.sync, qb_s, qb_scales, 0, 3)
+        load_scales(nc.sync, kb_s, kb_scales, 2, 4)
+
         for s in range(1, STEPS):
             load_ka(s)
             load_kb(s)
+        nc.sync.dma_start(out=cw_cols[:], in_=cw1.rearrange("o (h p j) -> p (o h) j", h=2, j=4))
+        nc.sync.dma_start(out=cw_first[:], in_=cw1[:, :QUARTER].partition_broadcast(P))
 
         nc.scalar.activation(out=mag[:, :, STEPS:], in_=ones[:], func=ACT.Copy, scale=0.1 / 0.7)
         cast_scalar(0)
         cast_vector(0)
         quantize(0)
-        nc.tensor.transpose(acc[2][1][:, :P], cw_rows[:], ident[:])
-        nc.scalar.copy(out=cw_cols[:], in_=acc[2][1][:, : I // P])
-        spread_cw(acc[3][1], 0, 2)
-        nc.scalar.copy(out=cw_first[:], in_=acc[3][1][:, :QUARTER])
         for t in range(TILES):
             pass_a(t, 0, True, False)
         for t in range(TILES):
@@ -250,8 +256,8 @@ def tile_mix_shares_by_row_scale_kernel(tc, qa_words, qa_scales, ka, qb_words, q
         row_max(2, last)
         exponential(0, 0)
         exponential(0, 1)
-        spread_cw(acc[0][0], 4, 4)
-        spread_cw(acc[0][1], 2, 2)
+        spread_cw(acc[0][0], 1)
+        spread_cw(acc[0][1], 0)
         denominator(1, 3)
         row_max(3, last)
         magnitude(3, last)
@@ -268,10 +274,10 @@ def tile_mix_shares_by_row_scale_kernel(tc, qa_words, qa_scales, ka, qb_words, q
         denominator(3, 4)
         weigh_first(0)
         shares_first(0)
-        shares(0, 1, 0, HALF, acc[0][0][:])
+        shares(0, 1, 0, HALF)
         store(0, 1, 0, HALF)
         sharpness(3, 4)
-        shares(0, 0, QUARTER, HALF, acc[0][1][:, :QUARTER])
+        shares(0, 0, QUARTER, HALF)
         store(0, 0, 0, HALF)
         add_halves(1)
         shifts(3, 4)
@@ -281,18 +287,18 @@ def tile_mix_shares_by_row_scale_kernel(tc, qa_words, qa_scales, ka, qb_words, q
         for t in (1, 2):
             weigh_first(t)
             shares_first(t)
-            shares(t, 1, 0, HALF, acc[0][0][:])
+            shares(t, 1, 0, HALF)
             store(t, 1, 0, HALF)
             add_halves(t + 1)
-            shares(t, 0, QUARTER, HALF, acc[0][1][:, :QUARTER])
+            shares(t, 0, QUARTER, HALF)
             store(t, 0, 0, HALF)
             invert(t + 1)
         t = TILES - 1
         weigh_first(t)
         shares_first(t)
         for g in range(2):
-            shares(t, 1, g * QUARTER, (g + 1) * QUARTER, acc[0][0][:, cols(g, QUARTER)])
+            shares(t, 1, g * QUARTER, (g + 1) * QUARTER)
             store(t, 1, g * QUARTER, (g + 1) * QUARTER)
         store(t, 0, 0, QUARTER)
-        shares(t, 0, QUARTER, HALF, acc[0][1][:, :QUARTER])
+        shares(t, 0, QUARTER, HALF)
         store(t, 0, QUARTER, HALF)

@@ -23,8 +23,12 @@ TILES = Q // P
 HALF = 512
 QUARTER = 256
 STEPS = I // QUARTER
+LAST_TILE = TILES - 1
+LAST_STEP = STEPS - 1
 B_PASSES = L // (P * PACK)
-SCALAR_COLS = (80, 96, 96, 96)
+SCALE_ROWS = 4
+CW_BLOCKS = HALF // P
+SCALAR_COLS = 96
 
 
 def tile_mix_shares_by_row_scale_kernel(tc, qa_words, qa_scales, ka, qb_words, qb_scales, kb_words, kb_scales, cw1, out):
@@ -45,11 +49,11 @@ def tile_mix_shares_by_row_scale_kernel(tc, qa_words, qa_scales, ka, qb_words, q
         ka_bf = [sb.tile([P, QUARTER, PACK], BF16, align_bytes=64, name="ka_bf_%d" % s) for s in range(STEPS)]
         ka_w = [sb.tile([P, QUARTER], U32, align_bytes=64, name="ka_w_%d" % s) for s in range(STEPS)]
         ka_s = [sb.tile([P, QUARTER], U8, align_bytes=64, name="ka_s_%d" % s) for s in range(STEPS)]
-        cw_cols = sb.tile([P, 2, 4], F32)
+        cw_cols = sb.tile([P, 2, CW_BLOCKS], F32)
         cw_first = sb.tile([P, QUARTER], F32)
         ident = sb.tile([P, P], F32)
+        zeros = sb.tile([P, TILES, 1], F32)
         ones = sb.tile([P, TILES, 1], F32)
-        warm = sb.tile([P, 1], F32)
         e = [[sb.tile([P, HALF], F32, name="e_%d_%d" % (t, h)) for h in range(2)] for t in range(TILES)]
         y = [[sb.tile([P, HALF], F32, name="y_%d_%d" % (t, h)) for h in range(2)] for t in range(TILES)]
         weighted = [sb.tile([P, QUARTER], F32, name="weighted_%d" % t) for t in range(TILES)]
@@ -72,9 +76,9 @@ def tile_mix_shares_by_row_scale_kernel(tc, qa_words, qa_scales, ka, qb_words, q
         def scores(t, s):
             return acc[t][s % 2][:, cols(s // 2, QUARTER)]
 
-        def load_scales(queue, plane, scales, first, last):
-            rows = scales.rearrange("z (q r) n -> r q z n", r=4)
-            for r in range(first, last):
+        def load_scales(queue, plane, scales, first, end):
+            rows = scales.rearrange("z (c r) n -> r c z n", r=SCALE_ROWS)
+            for r in range(first, end):
                 queue.dma_start(out=plane[r:P:32, :, :].bitcast(I32), in_=rows[r].bitcast(I32))
 
         def load_ka(s):
@@ -85,17 +89,12 @@ def tile_mix_shares_by_row_scale_kernel(tc, qa_words, qa_scales, ka, qb_words, q
         def load_kb(s):
             nc.sync.dma_start(out=kb_w[s][:].bitcast(I32), in_=kb_by_partition[:, :, cols(quarter(s), QUARTER)])
 
-        def interleave(copy, s, lo, hi):
-            copy(
-                out=ka_bf[s][:, lo:hi, :].rearrange("p (g w) j -> p g j w", w=4),
-                in_=ka_raw[s][:, :, lo:hi].rearrange("p j (g w) -> p g j w", w=4),
-            )
-
-        def cast_scalar(s):
-            interleave(nc.scalar.copy, s, 0, SCALAR_COLS[s])
-
-        def cast_vector(s):
-            interleave(nc.vector.tensor_copy, s, SCALAR_COLS[s], QUARTER)
+        def round_ka(s):
+            for copy, lo, hi in ((nc.scalar.copy, 0, SCALAR_COLS), (nc.vector.tensor_copy, SCALAR_COLS, QUARTER)):
+                copy(
+                    out=ka_bf[s][:, lo:hi, :].rearrange("p (g w) j -> p g j w", w=4),
+                    in_=ka_raw[s][:, :, lo:hi].rearrange("p j (g w) -> p g j w", w=4),
+                )
 
         def quantize(s):
             nc.vector.quantize_mx(out=ka_w[s][:].bitcast(FP8X4), scales=ka_s[s][:], in_=ka_bf[s][:].rearrange("p w j -> p (w j)"))
@@ -135,16 +134,11 @@ def tile_mix_shares_by_row_scale_kernel(tc, qa_words, qa_scales, ka, qb_words, q
         def denominator(lo, hi):
             nc.vector.tensor_reduce(out=denom[:, lo:hi], in_=mag[:, lo:hi, :], axis=AXIS.X, op=ALU.add)
 
+        def sharpness(lo, hi):
+            nc.vector.reciprocal(out=sharp[:, lo:hi], in_=denom[:, lo:hi])
+
         def join_maxima(lo, hi):
             nc.vector.tensor_reduce(out=neg_max_row[:, lo:hi], in_=neg_max[:, lo:hi, :], axis=AXIS.X, op=ALU.min)
-
-        def join_early_maxima(t):
-            nc.vector.tensor_reduce(out=neg_max_row[:, t : t + 1], in_=neg_max[:, t, : STEPS - 1], axis=AXIS.X, op=ALU.min)
-
-        def first_shift(t):
-            nc.vector.tensor_scalar(
-                out=shift[:, t : t + 1], in0=neg_max[:, t, STEPS - 1 :], scalar1=neg_max_row[:, t : t + 1], scalar2=sharp[:, t : t + 1], op0=ALU.min, op1=ALU.mult
-            )
 
         def shifts(lo, hi):
             for t in range(lo, hi):
@@ -152,13 +146,11 @@ def tile_mix_shares_by_row_scale_kernel(tc, qa_words, qa_scales, ka, qb_words, q
                     out=shift[:, t : t + 1], in0=neg_max_row[:, t : t + 1], scalar1=sharp[:, t : t + 1], scalar2=None, op0=ALU.mult
                 )
 
-        def sharpness(lo, hi):
-            nc.vector.reciprocal(out=sharp[:, lo:hi], in_=denom[:, lo:hi])
-
-        def exponential(t, h):
-            nc.scalar.activation(
-                out=e[t][h][:], in_=acc[t][h][:], func=ACT.Exp, scale=sharp[:, t : t + 1], bias=shift[:, t : t + 1], accum_out=esum[t][h][:]
-            )
+        def exponentials(t):
+            for h in range(2):
+                nc.scalar.activation(
+                    out=e[t][h][:], in_=acc[t][h][:], func=ACT.Exp, scale=sharp[:, t : t + 1], bias=shift[:, t : t + 1], accum_out=esum[t][h][:]
+                )
 
         def add_halves(t):
             nc.vector.tensor_scalar(
@@ -168,25 +160,26 @@ def tile_mix_shares_by_row_scale_kernel(tc, qa_words, qa_scales, ka, qb_words, q
         def invert(t):
             nc.vector.reciprocal(out=inv[t][:], in_=total[t][:])
 
-        def spread_cw(bank, h):
-            for j in range(4):
-                nc.tensor.transpose(bank[:, cols(j, P)], cw_cols[:, h, j : j + 1].to_broadcast([P, P]), ident[:])
+        def cw_bank(h):
+            return acc[0][1 - h]
+
+        def spread_cw(h):
+            for j in range(CW_BLOCKS):
+                nc.tensor.transpose(cw_bank(h)[:, cols(j, P)], cw_cols[:, h, j : j + 1].to_broadcast([P, P]), ident[:])
 
         def shares(t, h, lo, hi):
-            cw_bank = acc[0][1 - h][:].rearrange("p (j n) -> p n j", j=4)
+            weights = cw_bank(h)[:].rearrange("p (j n) -> p n j", j=CW_BLOCKS)
             nc.vector.scalar_tensor_tensor(
-                out=y[t][h][:, lo:hi].rearrange("p (n j) -> p n j", j=4),
-                in0=e[t][h][:, lo:hi].rearrange("p (n j) -> p n j", j=4),
+                out=y[t][h][:, lo:hi].rearrange("p (n j) -> p n j", j=CW_BLOCKS),
+                in0=e[t][h][:, lo:hi].rearrange("p (n j) -> p n j", j=CW_BLOCKS),
                 scalar=inv[t][:],
-                in1=cw_bank[:, lo // 4 : hi // 4, :],
+                in1=weights[:, lo // CW_BLOCKS : hi // CW_BLOCKS, :],
                 op0=ALU.mult,
                 op1=ALU.mult,
             )
 
-        def weigh_first(t):
+        def first_shares(t):
             nc.gpsimd.tensor_tensor(out=weighted[t][:], in0=e[t][0][:, :QUARTER], in1=cw_first[:], op=ALU.mult)
-
-        def shares_first(t):
             nc.gpsimd.tensor_scalar(
                 out=y[t][0][:, :QUARTER], in0=weighted[t][:], scalar1=inv[t][:], scalar2=0.0, op0=ALU.mult, op1=ALU.add
             )
@@ -194,111 +187,106 @@ def tile_mix_shares_by_row_scale_kernel(tc, qa_words, qa_scales, ka, qb_words, q
         def store(t, h, lo, hi):
             nc.sync.dma_start(out=out[cols(t, P), h * HALF + lo : h * HALF + hi], in_=y[t][h][:, lo:hi])
 
-        nc.gpsimd.memset(qb_s[:].bitcast(I32), 0)
-        for plane in (qa_s, kb_s):
+        nc.gpsimd.memset(kb_s[:].bitcast(I32), 0)
+        for plane in (qa_s, qb_s):
             nc.vector.memset(plane[:].bitcast(I32), 0)
-        load_scales(nc.gpsimd, qb_s, qb_scales, 3, 4)
+        load_scales(nc.gpsimd, kb_s, kb_scales, 3, 4)
         make_identity(nc, ident[:])
-        nc.vector.memset(ones[:], 1.0)
-        nc.scalar.activation(out=warm[:], in_=ones[:, 0, :], func=ACT.Exp)
+        nc.vector.memset(zeros[:], 0.0)
+        load_scales(nc.scalar, qa_s, qa_scales, 2, 4)
+        nc.scalar.activation(out=ones[:], in_=zeros[:], func=ACT.Exp)
 
         nc.sync.dma_start(out=qa_w[:].bitcast(I32), in_=qa_words.rearrange("z p n t -> p (z n t)").bitcast(I32))
-        load_scales(nc.sync, qa_s, qa_scales, 0, 4)
+        load_scales(nc.sync, qa_s, qa_scales, 0, 2)
         load_scales(nc.sync, kb_s, kb_scales, 0, 2)
         load_ka(0)
         load_kb(0)
         nc.sync.dma_start(out=qb_w[:].bitcast(I32), in_=qb_words.rearrange("z p b -> p z b").bitcast(I32))
-        load_scales(nc.sync, qb_s, qb_scales, 0, 3)
-        load_scales(nc.sync, kb_s, kb_scales, 2, 4)
-
+        load_scales(nc.sync, qb_s, qb_scales, 0, 4)
+        load_scales(nc.sync, kb_s, kb_scales, 2, 3)
         for s in range(1, STEPS):
             load_ka(s)
             load_kb(s)
-        nc.sync.dma_start(out=cw_cols[:], in_=cw1.rearrange("o (h p j) -> p (o h) j", h=2, j=4))
+        nc.sync.dma_start(out=cw_cols[:], in_=cw1.rearrange("o (h p j) -> p (o h) j", h=2, j=CW_BLOCKS))
         nc.sync.dma_start(out=cw_first[:], in_=cw1[:, :QUARTER].partition_broadcast(P))
 
         nc.scalar.activation(out=mag[:, :, STEPS:], in_=ones[:], func=ACT.Copy, scale=0.1 / 0.7)
-        cast_scalar(0)
-        cast_vector(0)
+
+        round_ka(0)
         quantize(0)
         for t in range(TILES):
             pass_a(t, 0, True, False)
         for t in range(TILES):
             passes_b(t, 0, False, True)
-        last = STEPS - 1
         for s in range(1, STEPS):
-            cast_scalar(s)
-            cast_vector(s)
+            round_ka(s)
             if s > 1:
-                row_max(3, s - 2)
+                row_max(LAST_TILE, s - 2)
             quantize(s)
             for t in range(TILES):
                 passes_b(t, s, True, False)
                 pass_a(t, s, False, True)
-            if s < last:
-                for t in range(TILES):
-                    magnitude(t, s - 1)
-                    if t < 3:
-                        row_max(t, s - 1)
-        for t in range(3):
-            magnitude(t, last - 1)
-            row_max(t, last - 1)
-        join_early_maxima(0)
-        magnitude(0, last)
+            for t in range(LAST_TILE):
+                magnitude(t, s - 1)
+                row_max(t, s - 1)
+            if s < LAST_STEP:
+                magnitude(LAST_TILE, s - 1)
+
+        nc.vector.tensor_reduce(out=neg_max_row[:, :1], in_=neg_max[:, 0, :LAST_STEP], axis=AXIS.X, op=ALU.min)
+        magnitude(0, LAST_STEP)
         denominator(0, 1)
-        row_max(0, last)
+        row_max(0, LAST_STEP)
         sharpness(0, 1)
-        magnitude(3, last - 1)
-        magnitude(1, last)
-        first_shift(0)
-        magnitude(2, last)
-        row_max(1, last)
-        row_max(2, last)
-        exponential(0, 0)
-        exponential(0, 1)
-        spread_cw(acc[0][0], 1)
-        spread_cw(acc[0][1], 0)
+        magnitude(LAST_TILE, LAST_STEP - 1)
+        magnitude(1, LAST_STEP)
+        nc.vector.tensor_scalar(
+            out=shift[:, :1], in0=neg_max[:, 0, LAST_STEP:], scalar1=neg_max_row[:, :1], scalar2=sharp[:, :1], op0=ALU.min, op1=ALU.mult
+        )
+        magnitude(2, LAST_STEP)
+        row_max(1, LAST_STEP)
+        row_max(2, LAST_STEP)
+        exponentials(0)
+        spread_cw(1)
+        spread_cw(0)
+
         denominator(1, 3)
-        row_max(3, last)
-        magnitude(3, last)
+        row_max(LAST_TILE, LAST_STEP)
+        magnitude(LAST_TILE, LAST_STEP)
         sharpness(1, 3)
         join_maxima(1, 3)
-        row_max(3, last - 1)
+        row_max(LAST_TILE, LAST_STEP - 1)
         shifts(1, 3)
-        for t in (1, 2):
-            exponential(t, 0)
-            exponential(t, 1)
+        exponentials(1)
+        exponentials(2)
+
         add_halves(0)
-        join_maxima(3, 4)
+        join_maxima(LAST_TILE, TILES)
         invert(0)
-        denominator(3, 4)
-        weigh_first(0)
-        shares_first(0)
+        denominator(LAST_TILE, TILES)
+        first_shares(0)
         shares(0, 1, 0, HALF)
         store(0, 1, 0, HALF)
-        sharpness(3, 4)
+        sharpness(LAST_TILE, TILES)
         shares(0, 0, QUARTER, HALF)
         store(0, 0, 0, HALF)
         add_halves(1)
-        shifts(3, 4)
+        shifts(LAST_TILE, TILES)
         invert(1)
-        exponential(3, 0)
-        exponential(3, 1)
+        exponentials(LAST_TILE)
+
         for t in (1, 2):
-            weigh_first(t)
-            shares_first(t)
+            first_shares(t)
             shares(t, 1, 0, HALF)
             store(t, 1, 0, HALF)
             add_halves(t + 1)
             shares(t, 0, QUARTER, HALF)
             store(t, 0, 0, HALF)
             invert(t + 1)
-        t = TILES - 1
-        weigh_first(t)
-        shares_first(t)
+
+        first_shares(LAST_TILE)
         for g in range(2):
-            shares(t, 1, g * QUARTER, (g + 1) * QUARTER)
-            store(t, 1, g * QUARTER, (g + 1) * QUARTER)
-        store(t, 0, 0, QUARTER)
-        shares(t, 0, QUARTER, HALF)
-        store(t, 0, QUARTER, HALF)
+            shares(LAST_TILE, 1, g * QUARTER, (g + 1) * QUARTER)
+            store(LAST_TILE, 1, g * QUARTER, (g + 1) * QUARTER)
+        store(LAST_TILE, 0, 0, QUARTER)
+        shares(LAST_TILE, 0, QUARTER, HALF)
+        store(LAST_TILE, 0, QUARTER, HALF)

from contextlib import ExitStack

import concourse.mybir as mybir
from concourse.masks import make_identity

K, L, Q, I = 512, 1024, 512, 1024
FLOPS = 2 * (K + L) * Q * I

F32 = mybir.dt.float32
BF16 = mybir.dt.bfloat16
I32 = mybir.dt.int32
U32 = mybir.dt.uint32
U8 = mybir.dt.uint8
FP8X4 = mybir.dt.float8_e4m3fn_x4
FP4X4 = mybir.dt.float4_e2m1fn_x4
ALU = mybir.AluOpType
ACT = mybir.ActivationFunctionType
AXIS = mybir.AxisListType

P = 128
PACK = 4
TILES = Q // P
HALF = 512
QUARTER = 256
STEPS = I // QUARTER
LAST_TILE = TILES - 1
LAST_STEP = STEPS - 1
B_PASSES = L // (P * PACK)
SCALE_ROWS = 4
CW_BLOCKS = HALF // P
SCALAR_COLS = 96


def tile_mix_shares_by_row_scale_kernel(tc, qa_words, qa_scales, ka, qb_words, qb_scales, kb_words, kb_scales, cw1, out):
    nc = tc.nc
    with ExitStack() as ctx:
        sb = ctx.enter_context(tc.tile_pool(name="sb", bufs=1))
        psum = ctx.enter_context(tc.psum_pool(name="psum", bufs=1))
        ctx.enter_context(tc.manual_schedule())

        acc = [[psum.tile([P, HALF], F32, name="acc_%d_%d" % (t, h)) for h in range(2)] for t in range(TILES)]
        qa_w = sb.tile([P, Q], U32, align_bytes=64)
        qa_s = sb.tile([P, 1, Q], U8, align_bytes=64)
        qb_w = sb.tile([P, B_PASSES, 2 * Q], U8, align_bytes=64)
        qb_s = sb.tile([P, B_PASSES, Q], U8, align_bytes=64)
        kb_s = sb.tile([P, B_PASSES, I], U8, align_bytes=64)
        kb_w = [sb.tile([P, B_PASSES, QUARTER], U32, align_bytes=64, name="kb_w_%d" % s) for s in range(STEPS)]
        ka_raw = [sb.tile([P, PACK, QUARTER], F32, name="ka_raw_%d" % s) for s in range(STEPS)]
        ka_bf = [sb.tile([P, QUARTER, PACK], BF16, align_bytes=64, name="ka_bf_%d" % s) for s in range(STEPS)]
        ka_w = [sb.tile([P, QUARTER], U32, align_bytes=64, name="ka_w_%d" % s) for s in range(STEPS)]
        ka_s = [sb.tile([P, QUARTER], U8, align_bytes=64, name="ka_s_%d" % s) for s in range(STEPS)]
        cw_cols = sb.tile([P, 2, CW_BLOCKS], F32)
        cw_first = sb.tile([P, QUARTER], F32)
        ident = sb.tile([P, P], F32)
        zeros = sb.tile([P, TILES, 1], F32)
        ones = sb.tile([P, TILES, 1], F32)
        e = [[sb.tile([P, HALF], F32, name="e_%d_%d" % (t, h)) for h in range(2)] for t in range(TILES)]
        y = [[sb.tile([P, HALF], F32, name="y_%d_%d" % (t, h)) for h in range(2)] for t in range(TILES)]
        weighted = [sb.tile([P, QUARTER], F32, name="weighted_%d" % t) for t in range(TILES)]
        mag = sb.tile([P, TILES, STEPS + 1], F32)
        neg_max = sb.tile([P, TILES, STEPS], F32)
        neg_max_row = sb.tile([P, TILES], F32)
        denom = sb.tile([P, TILES], F32)
        sharp = sb.tile([P, TILES], F32)
        shift = sb.tile([P, TILES], F32)
        esum = [[sb.tile([P, 1], F32, name="esum_%d_%d" % (t, h)) for h in range(2)] for t in range(TILES)]
        total = [sb.tile([P, 1], F32, name="total_%d" % t) for t in range(TILES)]
        inv = [sb.tile([P, 1], F32, name="inv_%d" % t) for t in range(TILES)]

        def cols(n, width):
            return slice(n * width, (n + 1) * width)

        def quarter(s):
            return 2 * (s % 2) + s // 2

        def scores(t, s):
            return acc[t][s % 2][:, cols(s // 2, QUARTER)]

        def load_scales(queue, plane, scales, first, end):
            rows = scales.rearrange("z (c r) n -> r c z n", r=SCALE_ROWS)
            for r in range(first, end):
                queue.dma_start(out=plane[r:P:32, :, :].bitcast(I32), in_=rows[r].bitcast(I32))

        def load_ka(s):
            nc.sync.dma_start(out=ka_raw[s][:], in_=ka[:, cols(quarter(s), QUARTER)].rearrange("(p j) w -> p j w", j=PACK))

        kb_by_partition = kb_words.rearrange("z p n t -> p z (n t)").bitcast(I32)

        def load_kb(s):
            nc.sync.dma_start(out=kb_w[s][:].bitcast(I32), in_=kb_by_partition[:, :, cols(quarter(s), QUARTER)])

        def round_ka(s):
            for copy, lo, hi in ((nc.scalar.copy, 0, SCALAR_COLS), (nc.vector.tensor_copy, SCALAR_COLS, QUARTER)):
                copy(
                    out=ka_bf[s][:, lo:hi, :].rearrange("p (g w) j -> p g j w", w=4),
                    in_=ka_raw[s][:, :, lo:hi].rearrange("p j (g w) -> p g j w", w=4),
                )

        def quantize(s):
            nc.vector.quantize_mx(out=ka_w[s][:].bitcast(FP8X4), scales=ka_s[s][:], in_=ka_bf[s][:].rearrange("p w j -> p (w j)"))

        def pass_a(t, s, start, stop):
            nc.tensor.matmul_mx(
                out=scores(t, s),
                lhsT=qa_w[:, cols(t, P)].bitcast(FP8X4),
                lhsT_scale=qa_s[:, 0, cols(t, P)],
                rhs=ka_w[s][:].bitcast(FP8X4),
                rhs_scale=ka_s[s][:],
                start=start,
                stop=stop,
            )

        def passes_b(t, s, start, stop):
            for z in range(B_PASSES):
                for u in range(2):
                    nc.tensor.matmul_mx(
                        out=scores(t, s)[:, cols(u, P)],
                        lhsT=qb_w[:, z, cols(t, 2 * P)].bitcast(FP4X4),
                        lhsT_scale=qb_s[:, z, cols(t, P)],
                        rhs=kb_w[s][:, z, cols(u, P)].bitcast(FP8X4),
                        rhs_scale=kb_s[:, z, cols(2 * quarter(s) + u, P)],
                        start=start and z == 0 and u == 0,
                        stop=stop and z == B_PASSES - 1 and u == 1,
                    )

        def magnitude(t, s):
            nc.scalar.activation(
                out=e[t][s % 2][:, cols(s // 2, QUARTER)], in_=scores(t, s), func=ACT.Abs, scale=1.0 / (0.7 * I), accum_out=mag[:, t, s : s + 1]
            )

        def row_max(t, s):
            nc.vector.tensor_reduce(out=neg_max[:, t, s : s + 1], in_=scores(t, s), axis=AXIS.X, op=ALU.max, negate=True)

        def denominator(lo, hi):
            nc.vector.tensor_reduce(out=denom[:, lo:hi], in_=mag[:, lo:hi, :], axis=AXIS.X, op=ALU.add)

        def sharpness(lo, hi):
            nc.vector.reciprocal(out=sharp[:, lo:hi], in_=denom[:, lo:hi])

        def join_maxima(lo, hi):
            nc.vector.tensor_reduce(out=neg_max_row[:, lo:hi], in_=neg_max[:, lo:hi, :], axis=AXIS.X, op=ALU.min)

        def shifts(lo, hi):
            for t in range(lo, hi):
                nc.vector.tensor_scalar(
                    out=shift[:, t : t + 1], in0=neg_max_row[:, t : t + 1], scalar1=sharp[:, t : t + 1], scalar2=None, op0=ALU.mult
                )

        def exponentials(t):
            for h in range(2):
                nc.scalar.activation(
                    out=e[t][h][:], in_=acc[t][h][:], func=ACT.Exp, scale=sharp[:, t : t + 1], bias=shift[:, t : t + 1], accum_out=esum[t][h][:]
                )

        def add_halves(t):
            nc.vector.tensor_scalar(
                out=total[t][:], in0=esum[t][1][:], scalar1=esum[t][0][:], scalar2=1.0 / 256.0, op0=ALU.add, op1=ALU.mult
            )

        def invert(t):
            nc.vector.reciprocal(out=inv[t][:], in_=total[t][:])

        def cw_bank(h):
            return acc[0][1 - h]

        def spread_cw(h):
            for j in range(CW_BLOCKS):
                nc.tensor.transpose(cw_bank(h)[:, cols(j, P)], cw_cols[:, h, j : j + 1].to_broadcast([P, P]), ident[:])

        def shares(t, h, lo, hi):
            weights = cw_bank(h)[:].rearrange("p (j n) -> p n j", j=CW_BLOCKS)
            nc.vector.scalar_tensor_tensor(
                out=y[t][h][:, lo:hi].rearrange("p (n j) -> p n j", j=CW_BLOCKS),
                in0=e[t][h][:, lo:hi].rearrange("p (n j) -> p n j", j=CW_BLOCKS),
                scalar=inv[t][:],
                in1=weights[:, lo // CW_BLOCKS : hi // CW_BLOCKS, :],
                op0=ALU.mult,
                op1=ALU.mult,
            )

        def first_shares(t):
            nc.gpsimd.tensor_tensor(out=weighted[t][:], in0=e[t][0][:, :QUARTER], in1=cw_first[:], op=ALU.mult)
            nc.gpsimd.tensor_scalar(
                out=y[t][0][:, :QUARTER], in0=weighted[t][:], scalar1=inv[t][:], scalar2=0.0, op0=ALU.mult, op1=ALU.add
            )

        def store(t, h, lo, hi):
            nc.sync.dma_start(out=out[cols(t, P), h * HALF + lo : h * HALF + hi], in_=y[t][h][:, lo:hi])

        nc.gpsimd.memset(kb_s[:].bitcast(I32), 0)
        for plane in (qa_s, qb_s):
            nc.vector.memset(plane[:].bitcast(I32), 0)
        load_scales(nc.gpsimd, kb_s, kb_scales, 3, 4)
        make_identity(nc, ident[:])
        nc.vector.memset(zeros[:], 0.0)
        load_scales(nc.scalar, qa_s, qa_scales, 2, 4)
        nc.scalar.activation(out=ones[:], in_=zeros[:], func=ACT.Exp)

        nc.sync.dma_start(out=qa_w[:].bitcast(I32), in_=qa_words.rearrange("z p n t -> p (z n t)").bitcast(I32))
        load_scales(nc.sync, qa_s, qa_scales, 0, 2)
        load_scales(nc.sync, kb_s, kb_scales, 0, 2)
        load_ka(0)
        load_kb(0)
        nc.sync.dma_start(out=qb_w[:].bitcast(I32), in_=qb_words.rearrange("z p b -> p z b").bitcast(I32))
        load_scales(nc.sync, qb_s, qb_scales, 0, 4)
        load_scales(nc.sync, kb_s, kb_scales, 2, 3)
        for s in range(1, STEPS):
            load_ka(s)
            load_kb(s)
        nc.sync.dma_start(out=cw_cols[:], in_=cw1.rearrange("o (h p j) -> p (o h) j", h=2, j=CW_BLOCKS))
        nc.sync.dma_start(out=cw_first[:], in_=cw1[:, :QUARTER].partition_broadcast(P))

        nc.scalar.activation(out=mag[:, :, STEPS:], in_=ones[:], func=ACT.Copy, scale=0.1 / 0.7)

        round_ka(0)
        quantize(0)
        for t in range(TILES):
            pass_a(t, 0, True, False)
        for t in range(TILES):
            passes_b(t, 0, False, True)
        for s in range(1, STEPS):
            round_ka(s)
            if s > 1:
                row_max(LAST_TILE, s - 2)
            quantize(s)
            for t in range(TILES):
                passes_b(t, s, True, False)
                pass_a(t, s, False, True)
            for t in range(LAST_TILE):
                magnitude(t, s - 1)
                row_max(t, s - 1)
            if s < LAST_STEP:
                magnitude(LAST_TILE, s - 1)

        nc.vector.tensor_reduce(out=neg_max_row[:, :1], in_=neg_max[:, 0, :LAST_STEP], axis=AXIS.X, op=ALU.min)
        magnitude(0, LAST_STEP)
        denominator(0, 1)
        row_max(0, LAST_STEP)
        sharpness(0, 1)
        magnitude(LAST_TILE, LAST_STEP - 1)
        magnitude(1, LAST_STEP)
        nc.vector.tensor_scalar(
            out=shift[:, :1], in0=neg_max[:, 0, LAST_STEP:], scalar1=neg_max_row[:, :1], scalar2=sharp[:, :1], op0=ALU.min, op1=ALU.mult
        )
        magnitude(2, LAST_STEP)
        row_max(1, LAST_STEP)
        row_max(2, LAST_STEP)
        exponentials(0)
        spread_cw(1)
        spread_cw(0)

        denominator(1, 3)
        row_max(LAST_TILE, LAST_STEP)
        magnitude(LAST_TILE, LAST_STEP)
        sharpness(1, 3)
        join_maxima(1, 3)
        row_max(LAST_TILE, LAST_STEP - 1)
        shifts(1, 3)
        exponentials(1)
        exponentials(2)

        add_halves(0)
        join_maxima(LAST_TILE, TILES)
        invert(0)
        denominator(LAST_TILE, TILES)
        first_shares(0)
        shares(0, 1, 0, HALF)
        store(0, 1, 0, HALF)
        sharpness(LAST_TILE, TILES)
        shares(0, 0, QUARTER, HALF)
        store(0, 0, 0, HALF)
        add_halves(1)
        shifts(LAST_TILE, TILES)
        invert(1)
        exponentials(LAST_TILE)

        for t in (1, 2):
            first_shares(t)
            shares(t, 1, 0, HALF)
            store(t, 1, 0, HALF)
            add_halves(t + 1)
            shares(t, 0, QUARTER, HALF)
            store(t, 0, 0, HALF)
            invert(t + 1)

        first_shares(LAST_TILE)
        for g in range(2):
            shares(LAST_TILE, 1, g * QUARTER, (g + 1) * QUARTER)
            store(LAST_TILE, 1, g * QUARTER, (g + 1) * QUARTER)
        store(LAST_TILE, 0, 0, QUARTER)
        shares(LAST_TILE, 0, QUARTER, HALF)
        store(LAST_TILE, 0, QUARTER, HALF)
